import numpy as np, ml_dtypes
CORES = [36,164,52,180,100,228,116,244]
N = 8
BF = ml_dtypes.bfloat16
def gentries(a):
    return np.ascontiguousarray(a.reshape(8, 16, -1).transpose(0, 2, 1)).reshape(8, -1)
def gtable(e):
    e = np.asarray(e); return np.ascontiguousarray(e.reshape(8, -1, 16).transpose(0, 2, 1)).reshape(128, -1).astype(np.int32)
NV, NT, NL, RO = 1280, 1280, 256, 3
def graphs(rng):
    tp = np.zeros((N, 8, 16, NT), np.int64); oc = np.zeros((N, 8, 16, NV), np.int64); c = 16 * NT // NV
    for n in range(N):
        for g in range(8):
            e = rng.permutation(16 * NT) % NV
            o = rng.permuted(np.argsort(e.astype(np.uint16), kind="stable").reshape(NV, c), axis=1)
            tp[n, g] = e.reshape(NT, 16).T; oc[n, g] = (o[:, np.arange(16) % c] // 16).T
    return tp, oc
def levels(rng, n):
    return np.floor(rng.random((N, 8, 16, n)) * rng.integers(65, 257, (N, 8, 1, n))).astype(np.int64)
def pack(dom, val, tp, oc, q):
    return {"dom": dom.reshape(N, 128, NV).astype(np.float32).astype(BF), "val": val.reshape(N, 128, NT).astype(np.float32).astype(BF),
            "tp": np.ascontiguousarray(tp.reshape(N, 128, NT)).astype(np.int32), "oc": np.ascontiguousarray(oc.reshape(N, 128, NV)).astype(np.int32), "q": np.stack([gtable(a) for a in q])}
def setup_inputs(rng):
    tp, oc = graphs(rng)
    return pack(levels(rng, NV), levels(rng, NT), tp, oc, rng.integers(0, NT, (N, 8, NL)))
def rolled(rng, n):
    base = rng.integers(0, 250, (N, 8, 16)); sh = rng.integers(0, 16, (N, 8, 1, n))
    x = np.take_along_axis(base, ((np.arange(16)[:, None] + sh) % 16).reshape(N, 8, 16 * n), 2).reshape(N, 8, 16, n)
    x[:, :, 3] += rng.random((N, 8, n)) < 0.1
    return x
def setup_inputs_ties(rng):
    tp, oc = graphs(rng)
    return pack(rolled(rng, NV), rolled(rng, NT), tp, oc, rng.integers(0, NT, (N, 8, NL)))
def setup_inputs_alike(rng):
    tp, oc = graphs(rng); dom = levels(rng, NV); val = levels(rng, NT); q = rng.integers(0, NT, (N, 8, NL))
    q[:, 0] = rng.integers(0, NT, (N, 1)); q[:, 1] = rng.choice(np.array([0, 5, NT - 1, NT - 2, NT // 2]), (N, NL)); q[:, 5] = rng.choice(np.array([0, NT - 1]), (N, NL))
    tp[:, 2] = tp[:, 2, :1]; oc[:, 3] = rng.choice(np.array([0, NT - 1]), (N, 16, NV)); tp[:, 4] = rng.choice(np.array([0, NV - 1, NV // 2]), (N, 16, NT))
    dom[:, 6, :, 7] = 255; np.put_along_axis(tp[:, 6], rng.integers(0, 16, (N, 1, NT)), 7, 1)
    q[:, 7] = 16 * np.argsort(rng.random((N, NT // 16)), axis=1)[:, np.arange(NL) % (NT // 16)] + rng.integers(0, 16, (N, 1))
    tp[:, 7] = 16 * (np.arange(NT) // 16 % (NV // 16)) + rng.integers(0, 16, (N, 1, 1))
    return pack(dom, val, tp, oc, q)
def setup_inputs_full(rng):
    p = np.argsort(rng.random((3, N, 8, NL)), axis=-1); cv = np.arange(NV); ct = np.arange(NT); dom = levels(rng, NV); val = levels(rng, NT)
    bt = rng.integers(0, NV // NL, (N, 8, 16, NT)); bo = rng.integers(0, NT // NL, (N, 8, 16, NV)); bq = rng.integers(0, NT // NL, (N, 8, NL))
    bt[:, 0] = 2 * rng.integers(0, NV // NL // 2, (N, 16, NT)) + (np.arange(N) % 2)[:, None, None]
    bt[:, 1] = rng.integers(0, NV // NL); bq[:, 1] = rng.integers(0, NT // NL); val[:, 1] //= 2
    lt = NT // NL // (RO + 1); lv = NV // NL // RO
    bq[:, 4] = rng.integers(0, lt, (N, NL))
    bt[:, 4] = lv * np.minimum(ct // NL // lt, RO - 1) + rng.integers(0, lv, (N, 16, NT))
    bo[:, 4] = lt * (np.minimum(cv // NL // lv, RO - 1) + 1) + rng.integers(0, lt, (N, 16, NV))
    tp = NL * bt + p[0][:, :, ct % NL][:, :, None, :]
    oc = NL * bo + p[1][:, :, cv % NL][:, :, None, :]
    q = NL * bq + p[2]
    tab = NL * rng.integers(0, NV // NL, (N, 16, NL // 2)) + np.arange(NL // 2)
    tp[:, 2] = np.take_along_axis(tab, (p[0][:, 2][:, ct % NL] // 2)[:, None, :], 2)
    k = (rng.integers(0, NL, (N, 1, NV)) + (NL // 16) * np.arange(16)[:, None]) % NL
    oc[:, 3] = np.take_along_axis(np.repeat(q[:, 3][:, None, :], 16, axis=1), k, 2)
    return pack(dom, val, tp, oc, q)
def setup_inputs_ends(rng):
    tp, oc = graphs(rng)
    dom = 255 * (rng.random((N, 8, 16, NV)) < rng.random((N, 8, 1, NV))).astype(np.int64); val = 255 * (rng.random((N, 8, 16, NT)) < 0.3 * rng.random((N, 8, 1, NT))).astype(np.int64)
    dom[:, 1] = 0; val[:, 2] = 0; val[:, 3] = 255; dom[:, 5] = 255
    dom[:, 4] *= rng.random((N, 1, NV)) < 0.1; val[:, 6] *= rng.random((N, 1, NT)) < 0.1
    dom[:, 7] = rng.integers(240, 256, (N, 16, NV)); val[:, 7] = rng.integers(240, 256, (N, 16, NT))
    return pack(dom, val, tp, oc, rng.integers(0, NT, (N, 8, NL)))
def uneven(rng, n):
    return np.floor(np.exp2(8 * rng.random((N, 8, 1, n)) - 2 * rng.random((N, 8, 16, 1))) * rng.random((N, 8, 16, n))).astype(np.int64)
def setup_inputs_spread(rng):
    tp, oc = graphs(rng)
    return pack(uneven(rng, NV), uneven(rng, NT), tp, oc, np.minimum((NT * rng.random((N, 8, NL)) ** 3).astype(np.int64), NT - 1))
def check_inputs(d):
    bad = []
    for k, hi in (("dom", 255), ("val", 255), ("tp", NV - 1), ("oc", NT - 1), ("q", NT - 1)):
        v = np.asarray(d[k]).astype(np.float64)
        if not (np.all(v >= 0) and np.all(v <= hi) and np.all(v == np.floor(v))): bad.append("range of " + k)
    return bad
def pick(a, ix):
    return np.take_along_axis(a, ix[:, :, None, :], 3)
def reference(dom, val, tp, oc, q):
    dm = dom.astype(np.float32).astype(np.int64).reshape(N, 8, 16, NV); vl = val.astype(np.float32).astype(np.int64).reshape(N, 8, 16, NT)
    tpl = tp.astype(np.int64).reshape(N, 8, 16, NT); occ = oc.astype(np.int64).reshape(N, 8, 16, NV)
    cur = np.stack([gentries(a) for a in q]).astype(np.int64)
    for t in range(RO):
        p = pick(tpl, cur)
        x = pick(dm, p.reshape(N, 8, 16 * NL)).reshape(N, 8, 16, 16, NL)
        best = np.argmax(np.add.reduce(x, axis=2), axis=2)
        a = np.take_along_axis(p, best[:, :, None, :], 2)[:, :, 0]
        np.put_along_axis(vl, cur[:, :, None, :], np.min(x, axis=3), 3)
        p = pick(occ, a)
        x = pick(vl, p.reshape(N, 8, 16 * NL)).reshape(N, 8, 16, 16, NL)
        m = np.minimum(pick(dm, a), np.max(x, axis=3))
        best = np.argmax(np.add.reduce(x, axis=2), axis=2)
        cur = np.take_along_axis(p, best[:, :, None, :], 2)[:, :, 0]
        np.put_along_axis(dm, a[:, :, None, :], m, 3)
        d = 1 + t % (N - 1); ain = np.roll(a, d, axis=0); got = np.roll(m, d, axis=0)
        np.put_along_axis(dm, ain[:, :, None, :], np.minimum(pick(dm, ain), got), 3)
    s = np.stack([np.add.reduce(dm, axis=3), np.add.reduce(vl, axis=3)], axis=-1)
    return {"yt": cur.astype(np.float32), "yv": m.reshape(N, 128, NL).astype(np.float32).astype(BF), "ys": s.reshape(N, 128, 2).astype(np.float32)}

from concourse.mybir import AluOpType as OP, AxisListType, ActivationFunctionType

NV, NL, RO = 1280, 256, 3
WIN = NV + 32
CFG = {
    "pieces": [(0, 4), (4, 6), (6, 8)],
    "share": [[[3], [3]], [[3], [3]], [[3], [3]]],
    "gam": 1.5, "sig": 3.8, "cy": 1.04, "pe": 0.55, "sync": 160.0, "far": 3200.0, "par": (500, 150, 300),
    "bias": {'dic0': -6000, 'in0': 3500, 'rec1': 3900, 'dia1': -3400, 'arc0': 1300, 'pia0': 7500, 'dia0': -4100, 'sca0': -4000,
             'po2': 2400, 'scc0': 5200, 'in1': 6700, 'ara0': -8900, 'po1': 400, 'rea0': 6400, 'xas0': 8500, 'm1': 6500,
             'arc8': 3300, 'xcv0': -3400, 'pga1': 7500, 'pia1': -3900, 'rea1': 9000, 'd1a': 9000, 'pic1': 8700, 'out': -8300,
             'xas1': -6800, 'ara8': 7900, 'pga0': -1600, 'm0': 1300, 'k': 700, 'dic1': 2700, 'po0': 8200, 'rec0': -2300,
             'in2': 6400, 'xcs1': 2200, 'm2': -200, 'pgc1': -700, 'sca1': -3500, 'pv': -1500, 'd1c': 3300, 'pgc0': -300,
             'xav0': 8300, 'pic0': 7500, 'd0c': -1000, 'da': -5000, 'd0a': 3600, 'xcs0': 5200, 'scc1': -1500},
}

SCRATCH = {}
for _dt, _names in (
        ("int32", "Q:16 TP:1280 OC:1280 PI:8 PB:8"),
        ("float32", "IT:1280 PF:8 PG:8 PW:40 KS0:384 KS1:384 AR:384 YT:256 YS:2 SP:2"),
        ("float16", "IF:128 QB:384 PHc:256 PHa:256"),
        ("uint16", "ZO:2 BL:24 YL:16 GLc:24 GLa:24 OFc:16 Pc:256 Pa:256 OFa0:16 OFa1:16 OFa2:16 OFr0:16 OFr1:16 OFr2:16"),
        ("bfloat16", "DOM:1312 VAL:1312 PR:640 I16:128 IN:128 PM:256 W:24 B:144 RB:768 INV:384 KC:384 ON:128 MN:512 MX:512 "
                     "Z0:272 Z1:272 HIc:256 HIa:256 Xc:4096 Xa:4096 SCc:4096 SCa:4096 D:32 E:384 TM:256 DA:256 YV:256 JK:1280 "
                     "MS0:256 MS1:256 MS2:256 MR0:256 MR1:256 MR2:256")):
    for _x in _names.split():
        SCRATCH[_x.split(":")[0]] = ("sbuf", [128, int(_x.split(":")[1])], _dt)
for _x in "pK0 pK1 pG0 pG1 pO pC pY".split():
    SCRATCH[_x] = ("psum", [128, 512], "float32")
SEMAPHORES = ["cv", "cs", "cp", "cg", "lq", "ltp", "ldom", "lval", "loc", "sent", "oyt", "oyv", "oys"]
SEMAPHORES += ["al%d" % _t for _t in range(RO)] + ["am%d_%d" % (_t, _k) for _t in range(RO) for _k in range(4)]
COPY = ActivationFunctionType.Copy


def list_schedule(nodes):
    n = len(nodes)
    preds, log = [], {}
    for i, nd in enumerate(nodes):
        p = {}
        for regs, wr in ((nd["r"], False), (nd["w"] + nd["far"], True)):
            for name, lo, hi in regs:
                for lo2, hi2, wr2, j in log.get(name, []):
                    if name[0] == "p" or ((wr or wr2) and lo < hi2 and lo2 < hi):
                        free_edge = (nd["e"] == "p" and nodes[j]["e"] == "p") or name == "seq"
                        p[j] = max(p.get(j, 0.0), 0.0 if free_edge else nodes[j]["lat"] + CFG["sync"])
        preds.append(p)
        for regs, wr in ((nd["r"], False), (nd["w"] + nd["far"], True)):
            for name, lo, hi in regs:
                old = [] if name[0] == "p" else [x for x in log.get(name, []) if not (wr and lo <= x[0] and x[1] <= hi)]
                log[name] = old + [(lo, hi, wr, i)]
    succs = [[] for _ in nodes]
    prio = [nd["cost"] + nd["lat"] for nd in nodes]
    for i in range(n - 1, -1, -1):
        for j, lat in preds[i].items():
            prio[j] = max(prio[j], nodes[j]["cost"] + lat + prio[i])
    for i, p in enumerate(preds):
        for j in p:
            succs[j].append(i)
    prio = [x + CFG["bias"].get(nd["tag"], 0) for x, nd in zip(prio, nodes)]
    look, slack, margin = CFG["par"]
    left = [len(p) for p in preds]
    ready, free, out = [0.0] * n, {}, []
    avail = [i for i in range(n) if left[i] == 0]
    while avail:
        start = {i: max(ready[i], free.get(nodes[i]["e"], 0.0)) for i in avail}
        first = min(avail, key=lambda i: (start[i], -prio[i]))
        e, t0 = nodes[first]["e"], start[first]
        near = [i for i in avail if nodes[i]["e"] == e and start[i] <= t0 + look]
        i = max(near, key=lambda i: (prio[i], -i))
        if start[i] > t0:
            fill = [j for j in near if start[j] < start[i] and (
                start[j] + nodes[j]["cost"] <= start[i] + slack or (start[j] <= t0 and prio[j] + margin >= prio[i]))]
            if fill:
                i = max(fill, key=lambda j: (prio[j], -j))
        free[e] = start[i] + nodes[i]["cost"]
        avail.remove(i)
        out.append(i)
        for s in succs[i]:
            ready[s] = max(ready[s], free[e] + preds[s][i])
            left[s] -= 1
            if left[s] == 0:
                avail.append(s)
    return out


def rank_program(g, core, T, topo):
    rank = T.rank_of(core)
    if rank is None:
        return
    n_ranks = len(T.cores)
    pieces = CFG["pieces"]
    queue = {"v": g.vector, "s": g.scalar, "p": g.tensor, "g": g, "y": g.sync}
    own_sem = {"v": "cv", "s": "cs", "p": "cp", "g": "cg"}
    nodes, landing, tag = [], [], ["k"]
    cy, V, S = CFG["cy"], g.vector, g.scalar

    def A(name, lo, hi, step=1, rows=None):
        r = slice(None) if rows is None else slice(rows[0], rows[1])
        ap = T[name][r, lo:hi] if step == 1 else T[name][r, lo:hi:step]
        return ap, (name, lo, hi), (hi - lo + step - 1) // step

    def col(name, j):
        return A(name, j, j + 1)

    def op(e, call, reads, writes, cost, **more):
        nd = {"e": e, "kind": "op", "call": call, "r": reads, "w": writes, "far": [], "cost": cost, "lat": 0.0, "tag": tag[0]}
        nd.update(more)
        nodes.append(nd)

    def dma(e, sem, out, in_, reads, writes, lat):
        op(e, lambda: queue[e].dma_start(out, in_), reads, writes, 60.0, kind="dma", sem=sem, lat=lat)

    def send(dst, src_core, sem, out, src):
        rid, pid = topo.addr(dst, core)
        op("g", lambda: g.remote_dma(out[0], src[0], T.sem[sem], T.sem["sent"], pid, rid, topo.mask(core, dst)),
           [src[1]], [], 900.0, kind="send", n=len(topo.engines(core, dst)), far=[out[1]], lat=CFG["far"] - 900.0)
        landing.append((out[1], sem, len(topo.engines(src_core, core))))

    def plain(n):
        return max(64.0, n) * cy

    def vcopy(out, in_, f=1.0):
        op("v", lambda: V.tensor_copy(out[0], in_[0]), [in_[1]], [out[1]], plain(f * out[2]))

    def vts(out, in0, s1, s2, op0, op1=None, f=1.0):
        reads = [in0[1]] + [x[1] for x in (s1, s2) if isinstance(x, tuple)]
        args = [out[0], in0[0]] + [x[0] if isinstance(x, tuple) else x for x in (s1, s2)] + [op0] + ([] if op1 is None else [op1])
        op("v", lambda: V.tensor_scalar(*args), reads, [out[1]], plain(f * out[2]))

    def vtt(out, in0, in1, o, f=1.0):
        op("v", lambda: V.tensor_tensor(out[0], in0[0], in1[0], o), [in0[1], in1[1]], [out[1]], plain(f * out[2]))

    def vset(out, c):
        op("v", lambda: V.memset(out[0], c), [], [out[1]], plain(0.5 * out[2]))

    def vscan(out, m, x, o0, o1, f):
        op("v", lambda: V.tensor_tensor_scan(out[0], m[0], x[0], 0.0, o0, o1), [m[1], x[1]], [out[1]], plain(f * out[2]))

    def gather(e, out, win, offs):
        call = (lambda: V.tensor_copy(out[0], win[0].indirect(offs[0]))) if e == "v" else (
            lambda: S.activation(out[0], win[0].indirect(offs[0]), COPY))
        op(e, call, [win[1], offs[1]], [out[1]], 70.0 + out[2] * CFG["gam"] * cy)

    def gmin(out, win, offs, in1):
        op("v", lambda: V.tensor_tensor(out[0], win[0].indirect(offs[0]), in1[0], OP.min),
           [win[1], offs[1], in1[1]], [out[1]], 60.0 + out[2] * CFG["gam"] * cy)

    def scatter(win, offs, in_):
        op("v", lambda: V.tensor_copy(win[0].indirect(offs[0]), in_[0]), [offs[1], in_[1]], [win[1]],
           60.0 + in_[2] * CFG["sig"] * cy)

    def mm(out, lhsT, rhs, start, stop):
        op("p", lambda: g.tensor.matmul(out[0], lhsT[0], rhs[0], start, stop), [lhsT[1], rhs[1]], [out[1]],
           max(64, rhs[2]) * CFG["pe"])

    def act(out, in_, acc=None):
        if acc is None:
            op("s", lambda: S.activation(out[0], in_[0], COPY), [in_[1]], [out[1]], plain(out[2]))
        else:
            op("s", lambda: S.activation(out[0], in_[0], COPY, accum_out=acc[0]), [in_[1]], [out[1], acc[1]], plain(out[2]))

    def iota(out, pattern, base):
        op("g", lambda: g.iota(out[0], pattern, base, 0, allow_small_or_imprecise_dtypes=True), [], [out[1]], 130.0 + 2 * cy * out[2])

    table = {"c": "DOM", "a": "VAL"}
    pointers = {"c": "TP", "a": "OC"}
    pv = [(part, v) for part in range(2) for v in range(2)]

    def gathers(k, mine):
        for h in range(2):
            bank, lo, up = "pK%d" % h, 128 * h, 128 * h + 128
            p, hi, ph = A("P" + k, lo, up), A("HI" + k, lo, up), A("PH" + k, lo, up)
            tag[0] = "pg%s%d" % (k, h)
            gather("v", p, A(pointers[k], 0, NV), A("GL" + k, 8 * h, 8 * h + 8))
            tag[0] = "di%s%d" % (k, h)
            vts(hi, p, 2048.0, None, OP.add, f=0.5)
            vcopy(ph, p, 0.5)
            mm(A(bank, 0, 384), A("ON", 0, 128, rows=(0, 33)), A("KC", 0, 384, rows=(0, 33)), True, False)
            mm(A(bank, 0, 128), hi, A("I16", 0, 128), False, False)
            mm(A(bank, 256, 384), ph, A("IF", 0, 128), False, False)
            mm(A(bank, 256, 384), hi, A("IN", 0, 128), False, False)
        o0, o1 = (OP.max, OP.min) if k == "c" else (OP.min, OP.max)
        for c in range(8):
            x = A("X" + k, 512 * c, 512 * c + 512)
            tag[0] = "x%s%s%d" % (k, "v" if c in mine else "s", c // 4)
            gather("v" if c in mine else "s", x, A(table[k], 0, NV), A("P" + k, 32 * c, 32 * c + 32))
            tag[0] = "sc%s%d" % (k, c // 4)
            vscan(A("SC" + k, 512 * c, 512 * c + 512), A("MN" if k == "c" else "MX", 0, 512), x, o0, o1, 0.5)
        for h in range(2):
            tag[0] = "pi%s%d" % (k, h)
            for i in range(16):
                mm(A("pK%d" % h, i, 384, 16), A("X" + k, 2048 * h + i, 2048 * h + 2048, 16), A("W", 0, 24), False, i == 15)
            vscan(A("KS%d" % h, 0, 384), A("MX", 0, 384), A("pK%d" % h, 0, 384), OP.min, OP.max, 1.0)
            vtt(A("D", 16 * h, 16 * h + 16), A("KS%d" % h, 15, 256, 16), A("KS%d" % h, 143, 384, 16), OP.subtract)

    def zview(h, part, v):
        lo = 128 * part + 8 - 8 * v
        return A("Z%d" % h, lo, lo + 128)

    def relist(k):
        for h in range(2):
            tag[0] = "re%s%d" % (k, h)
            scatter(A("Z%d" % h, 0, 272), A("ZO", 0, 1), A("D", 16 * h, 16 * h + 16))
            for n, (part, v) in enumerate(pv):
                lo = 384 * part + 128 * v
                mm(A("pG%d" % h, 0, 8), zview(h, part, v), A("RB", lo, lo + 128, 16), n == 0, n == 3)
            vcopy(A("GL" + k, 8 * h, 8 * h + 8), A("pG%d" % h, 0, 8))

    def distinct(k, name, first=False):
        tag[0] = "d0" + k
        mm(A("pO", 0, 384), A("IN", 0, 128), A("INV", 0, 384), True, False)
        if first:
            mm(A("pO", 0, 384), A("IF", 0, 128), A("QB", 0, 384), False, True)
            mm(A("pC", 0, 16), A("IF", 0, 128), A("QB", 0, 256, 16), True, False)
        else:
            vcopy(A("GL" + k, 16, 24), A("GL" + k, 1, 16, 2))
            for h in range(2):
                for n, (part, v) in enumerate(pv):
                    lo = 384 * part + 128 * v
                    mm(A("pO", 128 * h, 128 * h + 128), zview(h, part, v), A("RB", lo, lo + 128), False, False)
                    lo = 384 * part + 256 + 64 * v
                    mm(A("pO", 256 + 64 * h, 320 + 64 * h), zview(h, part, v), A("RB", lo, lo + 64), False, h == 1 and n == 3)
            mm(A("pC", 0, 16), A("IN", 0, 128), A("INV", 256, 272), True, False)
            for h in range(2):
                for part, v in pv:
                    lo = 384 * part + 128 * v
                    mm(A("pC", 8 * h, 8 * h + 8), zview(h, part, v), A("RB", lo, lo + 128, 16), False, False)
        for lo, hi in ((0, 8), (8, 24)):
            tag[0] = "ar%s%d" % (k, lo)
            gather("s", A("AR", 16 * lo, 16 * hi), A("IT", 0, NV), A("GL" + k, lo, hi))
        tag[0] = "d1" + k
        vtt(A("E", 0, 384), A("pO", 0, 384), A("AR", 0, 384), OP.is_equal)
        for r in range(16):
            b = A("B", 15 - r, 143 - r)
            mm(A("pC", 0, 16), b, A("E", r, 256, 16), False, False)
            mm(A("pC", 1, 16, 2), b, A("E", 256 + r, 384, 16), False, r == 15)
        vts(A(name, 0, 16, 2), A("pC", 0, 16, 2), col("PG", 0), None, OP.min)
        vts(A(name, 1, 16, 2), A("pC", 1, 16, 2), col("PG", 1), None, OP.min)

    def put(win, offs, b, src):
        scatter(A(win, 0, WIN), A(offs, 2 * b, 2 * b + 2), src)

    dma("s", "lq", T.Q[:], T.q[:], [], [("Q", 0, 16)], 2000.0)
    dma("y", "ltp", T.TP[:], T.tp[:], [], [("TP", 0, NV), ("turn", 0, 1), ("seq", 0, 1)], 4600.0)
    dma("y", "ldom", T.DOM[:, 0:NV], T.dom[:], [("seq", 0, 1)], [("DOM", 0, NV)], 6000.0)
    dma("y", "lval", T.VAL[:, 0:NV], T.val[:], [("turn", 0, 1)], [("VAL", 0, NV), ("seq", 1, 2)], 3000.0)
    dma("y", "loc", T.OC[:], T.oc[:], [("seq", 1, 2)], [("OC", 0, NV)], 5000.0)

    op("g", lambda: g.iota(T.PI[:, 0:2], [[128, 2]], 0, 1), [], [("PI", 0, 2), ("seq", 2, 3)], 140.0)
    iota(A("IT", 0, 160), [[1, 160]], 0)
    iota(A("PR", 384, 640), [[0, 16], [1, 16]], 0)
    iota(A("PW", 0, 24), [[0, 3], [16, 8]], 0)
    vset(A("KC", 0, 384, rows=(0, 33)), 0.0)
    iota(A("IT", 160, NV), [[1, NV - 160]], 160)
    nodes[-1]["r"] = [("seq", 2, 3)]
    iota(A("KC", 0, 256, rows=(0, 1)), [[0, 16], [-256, 16]], 3840)
    iota(A("KC", 256, 384, rows=(0, 1)), [[0, 8], [-256, 16]], 5888)
    iota(A("PR", 0, 256), [[8, 2], [1, 8], [0, 16]], 0)
    iota(A("PR", 256, 384), [[8, 2], [2, 4], [0, 16]], 0)
    iota(A("PW", 24, 40), [[128, 2], [1, 8]], 0)
    vset(A("KC", 0, 128, rows=(32, 33)), -120.0)
    vset(A("KC", 128, 384, rows=(32, 33)), 8.0)
    vset(A("MN", 0, 512), 0.0)
    vset(A("MX", 0, 512), float(2 ** 25))
    vset(A("ON", 0, 128, rows=(0, 33)), 1.0)
    vset(A("INV", 256, 384), 0.0)
    vset(A("Z0", 0, 272), 0.0)
    vset(A("Z1", 0, 272), 0.0)
    vset(A("DOM", NV, WIN), 0.0)
    vset(A("MN", 0, 512, 16), 256.0)
    vset(A("MX", 0, 512, 16), 0.0)
    vset(A("B", 0, 15), 0.0)
    for j, bits in ((0, 15), (1, 112), (4, 7), (5, 8), (6, 127)):
        vts(col("PB", j), col("PI", 0), bits, None, OP.bitwise_and)
    vts(A("PB", 2, 4), A("PI", 0, 2), 4, None, OP.arith_shift_right)
    vcopy(A("BL", 0, 16), A("IT", 0, 16))
    vcopy(A("BL", 16, 24), A("IT", 0, 16, 2))
    vcopy(A("PF", 0, 7), A("PB", 0, 7))
    vcopy(A("GLc", 0, 16), A("Q", 0, 16))
    vcopy(A("GLc", 16, 24), A("Q", 1, 16, 2))
    pm, pb, pp, it = col("PF", 0), col("PF", 1), col("PF", 6), A("IT", 0, 128)
    vts(A("IF", 0, 128), it, pp, None, OP.is_equal)
    vts(A("IN", 0, 128), it, pp, -1.0, OP.is_equal, OP.mult)
    vts(A("I16", 0, 128), it, pp, 0.0625, OP.is_equal, OP.mult)
    vts(A("INV", 0, 256), A("PR", 384, 640), pm, -4096.0, OP.is_le, OP.mult, f=0.5)
    gather("v", A("QB", 0, 384), A("Q", 0, 16), A("BL", 0, 24))
    vts(A("B", 15, 144), A("IT", 0, 129), pb, 2048.0, OP.is_equal, OP.mult)
    vts(A("PG", 0, 2), A("IT", 0, 32, 16), pm, float(NV), OP.add, OP.add)
    vts(A("W", 0, 24), A("PW", 0, 24), pb, 4096.0, OP.is_equal, OP.mult)
    vts(col("ZO", 0), pm, 16.0, col("PF", 3), OP.mult, OP.add)
    vts(A("RB", 0, 384), A("PR", 0, 384), pm, 16.0, OP.is_equal, OP.mult, f=0.5)
    vts(A("RB", 384, 768), A("PR", 0, 384), pm, -1.0, OP.is_equal, OP.mult, f=0.5)
    vts(col("PG", 2), col("PF", 4), 16.0, col("PF", 5), OP.mult, OP.add)
    vts(col("PG", 3), col("PG", 2), col("PF", 2), None, OP.add)
    vts(A("YL", 0, 16), A("PW", 24, 40), col("PG", 2), None, OP.add)
    vts(A("PM", 0, 128), it, col("PG", 3), 16.0, OP.is_equal, OP.mult)
    vts(A("PM", 128, 256), it, col("PG", 3), -1.0, OP.is_equal, OP.mult)

    distinct("c", "OFc", True)
    for t in range(RO):
        d = 1 + t % (n_ranks - 1)
        to, frm = T.cores[(rank + d) % n_ranks], T.cores[(rank - d) % n_ranks]
        ofa, ofr, ms, mr = "OFa%d" % t, "OFr%d" % t, "MS%d" % t, "MR%d" % t
        mine = CFG["share"][t][0]
        gathers("c", mine)
        tag[0] = "pv"
        for b in sorted(range(8), key=lambda b: b if b not in mine else (0.5 if b < 4 else b - 1.5)):
            put("VAL", "OFc", b, A("SCc", 512 * b + 15, 512 * b + 512, 16))
        relist("a")
        distinct("a", ofa)
        send(to, frm, "al%d" % t, A(ofr, 0, 16), A(ofa, 0, 16))
        gathers("a", CFG["share"][t][1])
        for k, (b0, b1) in enumerate(pieces):
            tag[0] = "m%d" % k
            m, top = A(ms, 32 * b0, 32 * b1), A("SCa", 512 * b0 + 15, 512 * b1, 16)
            if k == 0:
                gmin(m, A("DOM", 0, NV), A("GLa", 2 * b0, 2 * b1), top)
                tag[0] = "da"
                gather("s", A("DA", 32 * b1, NL), A("DOM", 0, NV), A("GLa", 2 * b1, 16))
            else:
                vtt(m, A("DA", 32 * b0, 32 * b1), top, OP.min, 2.0)
            send(to, frm, "am%d_%d" % (t, k), A(mr, 32 * b0, 32 * b1), m)
            tag[0] = "po%d" % k
            for b in range(b0, b1):
                put("DOM", ofa, b, A(ms, 32 * b, 32 * b + 32))
        if t < RO - 1:
            relist("c")
            distinct("c", "OFc")
        else:
            tag[0] = "out"
            for h, part in pv:
                mm(A("pY", 128 * h, 128 * h + 128, rows=(0, 8)), A("D", 16 * h + 8 * part, 16 * h + 8 * part + 8),
                   A("PM", 128 * part, 128 * part + 128), part == 0, part == 1)
            gather("s", A("YV", 0, NL), A(ms, 0, NL), A("YL", 0, 16))
            dma("y", "oyv", T.yv[:], T.YV[:], [("YV", 0, NL)], [], 2200.0)
            yt = A("YT", 0, NL, rows=(0, 8))
            act(yt, A("pY", 0, NL, rows=(0, 8)))
            dma("y", "oyt", T.yt[:], yt[0], [yt[1]], [], 2000.0)
            act(A("JK", 0, NV), A("VAL", 0, NV), col("YS", 1))
        for k, (b0, b1) in enumerate(pieces):
            tag[0] = "in%d" % k
            gmin(A("TM", 32 * b0, 32 * b1), A("DOM", 0, WIN), A(ofr, 2 * b0, 2 * b1), A(mr, 32 * b0, 32 * b1))
            for b in range(b0, b1):
                put("DOM", ofr, b, A("TM", 32 * b, 32 * b + 32))
    half = NV // 2
    act(A("JK", 0, half), A("DOM", 0, half), col("SP", 0))
    op("v", lambda: V.tensor_reduce(T.SP[:, 1:2], T.DOM[:, half:NV], AxisListType.X, OP.add),
       [("DOM", half, NV)], [("SP", 1, 2)], plain(half))
    vtt(col("YS", 0), col("SP", 0), col("SP", 1), OP.add)
    dma("y", "oys", T.ys[:], T.YS[:], [("YS", 0, 2)], [], 2000.0)

    total = {}
    known = {e: {} for e in queue}
    carried = {}
    log = {}
    for region, sem, n in landing:
        total[sem] = n
        log.setdefault(region[0], []).append((region[1], region[2], True, (sem, n), "dma"))

    def wait(e, tok):
        if known[e].get(tok[0], 0) < tok[1]:
            queue[e].wait_ge(T.sem[tok[0]], tok[1])
            known[e][tok[0]] = tok[1]
            for s2, n2 in carried.get(tok, {}).items():
                known[e][s2] = max(known[e].get(s2, 0), n2)

    for i in list_schedule(nodes):
        nd = nodes[i]
        e, need = nd["e"], {}
        for regs, wr in ((nd["r"], False), (nd["w"], True)):
            for name, lo, hi in regs:
                for lo2, hi2, wr2, tok, e2 in log.get(name, []):
                    hit = (wr or wr2) and lo < hi2 and lo2 < hi and name != "seq"
                    hit = (hit and e != "p") if e2 == e else (hit or name[0] == "p")
                    if hit and need.get(tok[0], 0) < tok[1]:
                        need[tok[0]] = tok[1]
        for s in sorted(need, key=lambda s: s == own_sem.get(e)):
            wait(e, (s, need[s]))
        if nd["kind"] == "send":
            nd["call"]()
            total["sent"] = total.get("sent", 0) + nd["n"]
            continue
        s, n, who = (own_sem[e], 1, e) if nd["kind"] == "op" else (nd["sem"], 16, "dma")
        total[s] = total.get(s, 0) + n
        nd["call"]().then_inc(T.sem[s], n)
        carried[(s, total[s])] = dict(known[e])
        for regs, wr in ((nd["r"], False), (nd["w"], True)):
            for name, lo, hi in regs:
                log.setdefault(name, []).append((lo, hi, wr, (s, total[s]), who))

    for s in total:
        if not any(known[e].get(s, 0) >= total[s] for e in known):
            wait("y" if s[0] == "o" else "g", (s, total[s]))
